import numpy as np
import ml_dtypes


def mxq(x, axis, fmt="e4m3"):
    dtype, down = {"e4m3": (ml_dtypes.float8_e4m3fn, 7), "e5m2": (ml_dtypes.float8_e5m2, 14)}[fmt]
    v = np.moveaxis(np.asarray(x, np.float32).astype(ml_dtypes.bfloat16).astype(np.float64), axis, -1)
    blocks = v.reshape(v.shape[:-1] + (-1, 32))
    amax = np.abs(blocks).max(-1, keepdims=True)
    byte = np.maximum(np.where(amax > 0, np.frexp(amax)[1] - 1 + 127, 0) - down, 1)
    scale = np.exp2(byte - 127.0)
    codes = (blocks / scale).astype(np.float32).astype(dtype).astype(np.float64)
    return np.moveaxis((codes * scale).reshape(v.shape), -1, axis)


WIDE = False


def mx_kscale(k):
    if not WIDE:
        return np.ones(k)
    levels = np.array([10, -10, 5, -5, 0])
    if k % 512:
        return np.exp2(np.random.permutation(np.resize(levels, k // 32))).repeat(32)
    a = np.empty((k // 512, 16))
    for p in range(k // 512):
        a[p, :8] = np.random.permutation(np.resize(levels, 8))
        for g in range(8):
            far = levels[np.abs(levels - a[p, g]) >= 10]
            a[p, g + 8] = far[np.random.randint(len(far))]
    return np.exp2(a.ravel()).repeat(32)


def f64(x):
    return np.asarray(x).astype(np.float64)


def striped(idx):
    return np.tile(np.asarray(idx).reshape(-1, 16).T, (8, 1)).astype(np.uint16)


def unstriped(offs):
    return offs[:16].T.reshape(-1).astype(np.int64)


def striped8(idx):
    return np.asarray(idx).reshape(8, -1, 16).transpose(0, 2, 1).reshape(128, -1).astype(np.uint16)


def unstriped8(offs):
    return offs.reshape(8, 16, -1).transpose(0, 2, 1).reshape(8, -1).astype(np.int64)


def pick8(x, idx, run):
    r = np.arange(len(x))
    return x[r[:, None], idx[r % (8 * run) // run]]


E2M1 = np.array([0.0, 0.5, 1.0, 1.5, 2.0, 3.0, 4.0, 6.0, -0.0, -0.5, -1.0, -1.5, -2.0, -3.0, -4.0, -6.0])


def pack_weight(w, fmt):
    k, n = w.shape
    w = f64(np.asarray(w, np.float32).astype(ml_dtypes.bfloat16)).reshape(k // 32, 32, n)
    amax = np.abs(w).max(1)
    if fmt == "e4m3":
        byte = np.frexp(amax)[1] - 1 + 127 - 7
    else:
        mant, ex = np.frexp(amax / 6.0)
        byte = np.where(mant > 0.5, ex, ex - 1) + 127
    byte = np.clip(np.where(amax > 0, byte, 1), 1, 254)
    scaled = (w * np.exp2(127.0 - byte)[:, None, :]).reshape(k, n).astype(np.float32)
    by_word = np.ascontiguousarray(scaled.reshape(k // 512, 128, 4, n).transpose(0, 1, 3, 2))
    if fmt == "e4m3":
        words = by_word.astype(ml_dtypes.float8_e4m3fn).view(np.uint8)
    else:
        c = by_word.astype(ml_dtypes.float4_e2m1fn).view(np.uint8) & 0xF
        words = (c[..., 0::2] | (c[..., 1::2] << 4)).reshape(k // 512, 128, 2 * n)
    return np.ascontiguousarray(words), np.ascontiguousarray(byte.astype(np.uint8).reshape(k // 512, 16, n))


def unpack_weight(words, scales, fmt):
    g, _, n = scales.shape
    words = np.ascontiguousarray(words).reshape(g, 128, n, -1)
    if fmt == "e4m3":
        vals = words.view(ml_dtypes.float8_e4m3fn).astype(np.float64)
    else:
        nib = np.empty((g, 128, n, 4), np.uint8)
        nib[..., 0::2] = words & 0xF
        nib[..., 1::2] = words >> 4
        vals = E2M1[nib]
    vals = vals * np.repeat(np.exp2(scales.astype(np.float64) - 127.0), 8, axis=1)[..., None]
    return vals.transpose(0, 1, 3, 2).reshape(g * 512, n)


K, J, R, T, F, O, C, S, N, U = 512, 512, 512, 2048, 1024, 256, 512, 256, 256, 128


def setup_inputs():
    n = np.random.standard_normal
    idx = np.stack([np.random.permutation(T)[:J] for _ in range(8)])
    idx2 = np.random.permutation(F)[:R]
    idx3 = np.stack([np.random.permutation(J)[:S] for _ in range(8)])
    idx4 = np.stack([np.random.permutation(C)[:S] for _ in range(8)])
    idx5 = np.stack([np.random.permutation(C)[:O] for _ in range(8)])
    idx6 = np.stack([np.random.permutation(O)[:U] for _ in range(8)])
    idx7 = np.stack([np.random.permutation(O)[:U] for _ in range(8)])
    fk = mx_kscale(K)
    fr = mx_kscale(R)
    tr = np.ones(F)
    tr[idx2] = fr
    wtp = pack_weight(n((K, F)) * 1 / np.sqrt(K) / fk[:, None] * tr, "e2m1")
    wbp = pack_weight(n((R, N)) * 1 / np.sqrt(R) / fr[:, None], "e4m3")
    wop = pack_weight(n((R, N)) * 1 / np.sqrt(R) / fr[:, None], "e2m1")
    return {
        "ta": (np.random.randint(-7, 8, (K, T)).astype(np.float64)).astype(np.float32),
        "ga": ((np.random.randint(8, 25, (K, 1)) / 64.0) * fk[:, None]).astype(np.float32),
        "wt_words": wtp[0],
        "wt_scales": wtp[1],
        "sa": (np.random.uniform(0.5, 1.6, (R, 1))).astype(np.float32),
        "sb": (np.random.uniform(0.5, 1.6, (R, 1))).astype(np.float32),
        "wb_words": wbp[0],
        "wb_scales": wbp[1],
        "wo_words": wop[0],
        "wo_scales": wop[1],
        "so": (np.random.uniform(0.5, 1.6, (N, 1))).astype(np.float32),
        "sp": (np.random.uniform(0.5, 1.6, (N, 1))).astype(np.float32),
        "offs": striped8(idx),
        "offs2": striped(idx2),
        "offs3": striped8(idx3),
        "offs4": striped8(idx4),
        "offs5": striped8(idx5),
        "offs6": striped8(idx6),
        "offs7": striped8(idx7),
    }


def reference(ta, ga, wt_words, wt_scales, sa, sb, wb_words, wb_scales, wo_words, wo_scales, so, sp, offs, offs2, offs3, offs4, offs5, offs6, offs7):
    idx = unstriped8(offs)
    idx2 = unstriped(offs2)
    idx3 = unstriped8(offs3)
    idx4 = unstriped8(offs4)
    idx5 = unstriped8(offs5)
    idx6 = unstriped8(offs6)
    idx7 = unstriped8(offs7)
    wtu = unpack_weight(wt_words, wt_scales, "e2m1")
    wbu = unpack_weight(wb_words, wb_scales, "e4m3")
    wou = unpack_weight(wo_words, wo_scales, "e2m1")
    xc = pick8(f64(ta), idx, 64) * f64(ga)
    wtidx2g = wtu[:, idx2]
    xcq = mxq(xc, 0, "e4m3")
    a = wtidx2g.T @ xcq
    h1 = pick8(a, idx3, 64) * f64(sa)
    pw = np.zeros((R, C))
    pw[np.arange(R)[:, None], idx4[np.arange(R) % 512 // 64]] = h1
    g1 = np.maximum(pw, 0.0)
    hid = pick8(g1, idx5, 64) * f64(sb)
    hidq = mxq(hid, 0, "e4m3")
    p = wbu.T @ hidq
    q = wou.T @ hidq
    y = pick8(p, idx6, 16) * f64(so) - pick8(q, idx7, 16) * f64(sp)
    return y

@@ -1,0 +1,213 @@
+from contextlib import ExitStack
+
+import concourse.mybir as mybir
+
+K, J, R, T, F, O, C, S, N, U = 512, 512, 512, 2048, 1024, 256, 512, 256, 256, 128
+FLOPS = 2 * K * R * J + 2 * 2 * R * N * O
+
+F32 = mybir.dt.float32
+BF16 = mybir.dt.bfloat16
+I32 = mybir.dt.int32
+U32 = mybir.dt.uint32
+U16 = mybir.dt.uint16
+U8 = mybir.dt.uint8
+FP8X4 = mybir.dt.float8_e4m3fn_x4
+FP4X4 = mybir.dt.float4_e2m1fn_x4
+ACT = mybir.ActivationFunctionType
+ALU = mybir.AluOpType
+
+P = 128
+PACK = 4
+JH = J // 2
+SH = S // 2
+OH = O // 2
+
+
+def tile_picked_codes_store_one_weighedposting_outcomes_outmeet_kernel(
+    tc, ta, ga, wt_words, wt_scales, sa, sb, wb_words, wb_scales, wo_words, wo_scales, so, sp,
+    offs, offs2, offs3, offs4, offs5, offs6, offs7, out
+):
+    nc = tc.nc
+    with ExitStack() as ctx:
+        sb_pool = ctx.enter_context(tc.tile_pool(name="keep", bufs=1))
+        psum = ctx.enter_context(tc.psum_pool(name="psum", bufs=1))
+
+        def tile(shape, dtype, name, tag=""):
+            return sb_pool.tile(shape, dtype, name=name, tag=tag, align_bytes=64)
+
+        def load_list(src, name):
+            lst = tile(list(src.shape), U16, name)
+            nc.sync.dma_start(lst[:], src)
+            return lst
+
+        def load_rows4(src, name):
+            col = tile([P, PACK], F32, name)
+            nc.sync.dma_start(col[:], src.rearrange("(p t) o -> p (t o)", t=PACK))
+            return col
+
+        def load_blocks2(src, name):
+            col = tile([P, 2], F32, name)
+            with nc.allow_non_contiguous_dma(reason="one value a partition and block"):
+                nc.sync.dma_start(col[:], src.rearrange("(b p) o -> p (b o)", b=2))
+            return col
+
+        ta_rows = ta.rearrange("(p t) c -> t p c", t=PACK)
+        ta_sb = [tile([P, T], F32, "ta%d" % t) for t in range(PACK)]
+
+        wts_win = tile([P, F], U8, "wts_win")
+        nc.vector.memset(wts_win[:].bitcast(I32), 0)
+        wbs = tile([P, N], U8, "wbs")
+        nc.vector.memset(wbs[:].bitcast(I32), 0)
+        wos = tile([P, N], U8, "wos")
+        nc.vector.memset(wos[:].bitcast(I32), 0)
+        board = [tile([P, C], F32, "board%d" % t, tag="board%d" % t) for t in range(PACK)]
+        for t in range(PACK):
+            nc.vector.memset(board[t][:], 0.0)
+
+        nc.sync.dma_start(ta_sb[0][:], ta_rows[0])
+        l1 = load_list(offs, "l1")
+        ga_sb = load_rows4(ga, "ga_sb")
+        nc.sync.dma_start(ta_sb[1][:], ta_rows[1])
+        wtw_win = tile([P, F], U16, "wtw_win")
+        nc.sync.dma_start(wtw_win[:].bitcast(I32), wt_words[0].bitcast(I32))
+        l2 = load_list(offs2, "l2")
+        wts_stage = tile([P, 2, F // 4], I32, "wts_stage")
+        wts_src = wt_scales[0].bitcast(I32).rearrange("(g q r) c -> g r q c", g=2, q=2)
+        for g in range(2):
+            nc.sync.dma_start(wts_stage[64 * g : 64 * g + 4], wts_src[g])
+        nc.sync.dma_start(ta_sb[2][:], ta_rows[2])
+        nc.sync.dma_start(ta_sb[3][:], ta_rows[3])
+        l3 = load_list(offs3, "l3")
+        sa_sb = load_rows4(sa, "sa_sb")
+        l4 = load_list(offs4, "l4")
+        l5 = load_list(offs5, "l5")
+        sb_sb = load_rows4(sb, "sb_sb")
+        wbw = tile([P, N], U32, "wbw")
+        nc.sync.dma_start(wbw[:].bitcast(I32), wb_words[0].rearrange("p n t -> p (n t)").bitcast(I32))
+        wow = tile([P, 2 * N], U8, "wow")
+        nc.sync.dma_start(wow[:].bitcast(I32), wo_words[0].bitcast(I32))
+        for plane, src in ((wbs, wb_scales), (wos, wo_scales)):
+            for q in range(4):
+                nc.sync.dma_start(plane[32 * q : 32 * q + 4, :].bitcast(I32), src[0, 4 * q : 4 * q + 4, :].bitcast(I32))
+        l6 = load_list(offs6, "l6")
+        l7 = load_list(offs7, "l7")
+        so_sb = load_blocks2(so, "so_sb")
+        sp_sb = load_blocks2(sp, "sp_sb")
+
+        for q in range(4):
+            first = 64 * (q // 2)
+            nc.vector.tensor_copy(wts_win[32 * q : 32 * q + 4, :].bitcast(I32), wts_stage[first : first + 4, q % 2, :])
+        wtw_g = tile([P, R], U16, "wtw_g")
+        nc.vector.tensor_copy(wtw_g[:], wtw_win[:].indirect(l2[:]))
+        wts_g = tile([P, R], U8, "wts_g")
+        nc.vector.tensor_copy(wts_g[:], wts_win[:].indirect(l2[:]))
+        wtw = tile([P, 2 * R], U8, "wtw")
+        nc.vector.tensor_copy(
+            wtw[:].rearrange("p (t m b) -> p t m b", t=PACK, b=2),
+            wtw_g[:].bitcast(U8).rearrange("p (m t b) -> p t m b", t=PACK, b=2),
+        )
+        wts = tile([P, R], U8, "wts")
+        nc.vector.tensor_copy(
+            wts[:].rearrange("p (t m) -> p t m", t=PACK),
+            wts_g[:].rearrange("p (m t) -> p t m", t=PACK),
+        )
+
+        xg_early = tile([P, PACK - 1, J], BF16, "xg_early")
+        xg_last = tile([P, J], BF16, "xg_last")
+        xi = [tile([P, JH, PACK], BF16, "xi%d" % h) for h in range(2)]
+        for t in range(PACK - 1):
+            nc.scalar.activation(xg_early[:, t, :], ta_sb[t][:].indirect(l1[:]), ACT.Copy, scale=ga_sb[:, t : t + 1])
+        for h in range(2):
+            nc.vector.tensor_copy(
+                xi[h][:, :, 0 : PACK - 1], xg_early[:, :, h * JH : (h + 1) * JH].rearrange("p t j -> p j t")
+            )
+        nc.scalar.activation(xg_last[:], ta_sb[PACK - 1][:].indirect(l1[:]), ACT.Copy, scale=ga_sb[:, PACK - 1 : PACK])
+        for h in range(2):
+            nc.vector.tensor_copy(xi[h][:, :, PACK - 1], xg_last[:, h * JH : (h + 1) * JH])
+        xq = tile([P, J], U32, "xq")
+        xs = tile([P, J], U8, "xs")
+        for h in range(2):
+            cols = slice(h * JH, (h + 1) * JH)
+            nc.vector.quantize_mx(xq[:, cols].bitcast(FP8X4), xs[:, cols], xi[h][:].rearrange("p j t -> p (j t)"))
+
+        a_sb = [tile([P, J], F32, "a%d" % t, tag="a%d" % t) for t in range(PACK)]
+
+        def first_product(t, cols, bank):
+            acc = psum.tile([P, cols.stop - cols.start], F32, name="a_ps", tag="bank%d" % bank)
+            nc.tensor.matmul_mx(
+                acc[:],
+                lhsT=wtw[:, 2 * P * t : 2 * P * (t + 1)].bitcast(FP4X4),
+                lhsT_scale=wts[:, P * t : P * (t + 1)],
+                rhs=xq[:, cols].bitcast(FP8X4),
+                rhs_scale=xs[:, cols],
+                start=True,
+                stop=True,
+            )
+            return acc
+
+        nc.scalar.copy(a_sb[0][:, 0:JH], first_product(0, slice(0, JH), 0)[:])
+        nc.vector.tensor_copy(a_sb[0][:, JH:J], first_product(0, slice(JH, J), 1)[:])
+        nc.vector.tensor_copy(a_sb[1][:], first_product(1, slice(0, J), 2)[:])
+        late = {t: first_product(t, slice(0, J), t + 1) for t in (2, 3)}
+
+        h1 = [tile([P, S], F32, "h1_%d" % t, tag="h1_%d" % t) for t in range(PACK)]
+        for t in range(PACK):
+            if t in late:
+                nc.scalar.copy(a_sb[t][:], late[t][:])
+            nc.scalar.activation(h1[t][:], a_sb[t][:].indirect(l3[:]), ACT.Copy, scale=sa_sb[:, t : t + 1])
+            src = h1[t]
+            if t in late:
+                src = tile([P, S], F32, "kept%d" % t)
+                nc.scalar.activation(src[:], h1[t][:], ACT.Relu)
+            nc.vector.tensor_copy(board[t][:].indirect(l4[:]), src[:])
+        g1 = []
+        for t, tag in ((0, "a3"), (1, "h1_3")):
+            g1.append(tile([P, C], F32, "g1_%d" % t, tag=tag))
+            nc.scalar.activation(g1[t][:], board[t][:], ACT.Relu)
+        g1.extend(board[2:])
+        hg_both = tile([P, 2, PACK, OH], BF16, "hg", tag="board1")
+        hg = [hg_both[:, h] for h in range(2)]
+        for t in range(PACK):
+            for h in range(2):
+                nc.scalar.activation(
+                    hg[h][:, t, :],
+                    g1[t][:].indirect(l5[:, h * OH // 16 : (h + 1) * OH // 16]),
+                    ACT.Copy,
+                    scale=sb_sb[:, t : t + 1],
+                )
+
+        hi_ = [tile([P, OH, PACK], BF16, "hi%d" % h) for h in range(2)]
+        hq = tile([P, O], U32, "hq")
+        hs = tile([P, O], U8, "hs")
+        for h in range(2):
+            nc.vector.tensor_copy(hi_[h][:], hg[h].rearrange("p t o -> p o t"))
+        for h in range(2):
+            cols = slice(h * OH, (h + 1) * OH)
+            nc.vector.quantize_mx(hq[:, cols].bitcast(FP8X4), hs[:, cols], hi_[h][:].rearrange("p o t -> p (o t)"))
+
+        for b in range(2):
+            sides = (
+                (wbw[:, P * b : P * (b + 1)].bitcast(FP8X4), wbs, l6, so_sb),
+                (wow[:, 2 * P * b : 2 * P * (b + 1)].bitcast(FP4X4), wos, l7, sp_sb),
+            )
+            picked = []
+            for m, (codes, plane, lst, weight) in enumerate(sides):
+                acc = psum.tile([P, O], F32, name="pq_ps", tag="bank%d" % ((5 + 2 * b + m) % 8))
+                for cols in (slice(0, OH), slice(OH, O)) if b == 0 else (slice(0, O),):
+                    nc.tensor.matmul_mx(
+                        acc[:, cols],
+                        lhsT=codes,
+                        lhsT_scale=plane[:, P * b : P * (b + 1)],
+                        rhs=hq[:, cols].bitcast(FP8X4),
+                        rhs_scale=hs[:, cols],
+                        start=True,
+                        stop=True,
+                    )
+                whole = tile([P, O], F32, "pq%d%d" % (b, m))
+                nc.vector.tensor_copy(whole[:], acc[:])
+                part = tile([P, U], F32, "picked%d%d" % (b, m))
+                nc.scalar.activation(part[:], whole[:].indirect(lst[:]), ACT.Copy, scale=weight[:, b : b + 1])
+                picked.append(part)
+            y = tile([P, U], F32, "y%d" % b)
+            nc.vector.tensor_tensor(y[:], picked[0][:], picked[1][:], ALU.subtract)
+            nc.sync.dma_start(out[P * b : P * (b + 1), :], y[:])

@@ -19,6 +19,7 @@ ALU = mybir.AluOpType
 P = 128
 PACK = 4
 JH = J // 2
+JQ = J // 4
 SH = S // 2
 OH = O // 2
 
@@ -67,7 +68,6 @@ def tile_picked_codes_store_one_weighedposting_outcomes_outmeet_kernel(
         nc.sync.dma_start(ta_sb[0][:], ta_rows[0])
         l1 = load_list(offs, "l1")
         ga_sb = load_rows4(ga, "ga_sb")
-        nc.sync.dma_start(ta_sb[1][:], ta_rows[1])
         wtw_win = tile([P, F], U16, "wtw_win")
         nc.sync.dma_start(wtw_win[:].bitcast(I32), wt_words[0].bitcast(I32))
         l2 = load_list(offs2, "l2")
@@ -75,6 +75,7 @@ def tile_picked_codes_store_one_weighedposting_outcomes_outmeet_kernel(
         wts_src = wt_scales[0].bitcast(I32).rearrange("(g q r) c -> g r q c", g=2, q=2)
         for g in range(2):
             nc.sync.dma_start(wts_stage[64 * g : 64 * g + 4], wts_src[g])
+        nc.sync.dma_start(ta_sb[1][:], ta_rows[1])
         nc.sync.dma_start(ta_sb[2][:], ta_rows[2])
         nc.sync.dma_start(ta_sb[3][:], ta_rows[3])
         l3 = load_list(offs3, "l3")
@@ -112,30 +113,39 @@ def tile_picked_codes_store_one_weighedposting_outcomes_outmeet_kernel(
             wts_g[:].rearrange("p (m t) -> p t m", t=PACK),
         )
 
-        xg_early = tile([P, PACK - 1, J], BF16, "xg_early")
-        xg_last = tile([P, J], BF16, "xg_last")
-        xi = [tile([P, JH, PACK], BF16, "xi%d" % h) for h in range(2)]
-        for t in range(PACK - 1):
-            nc.scalar.activation(xg_early[:, t, :], ta_sb[t][:].indirect(l1[:]), ACT.Copy, scale=ga_sb[:, t : t + 1])
-        for h in range(2):
-            nc.vector.tensor_copy(
-                xi[h][:, :, 0 : PACK - 1], xg_early[:, :, h * JH : (h + 1) * JH].rearrange("p t j -> p j t")
-            )
-        nc.scalar.activation(xg_last[:], ta_sb[PACK - 1][:].indirect(l1[:]), ACT.Copy, scale=ga_sb[:, PACK - 1 : PACK])
-        for h in range(2):
-            nc.vector.tensor_copy(xi[h][:, :, PACK - 1], xg_last[:, h * JH : (h + 1) * JH])
+        pieces = [slice(i * JQ, (i + 1) * JQ) for i in range(4)]
+        xg = [tile([P, 2, J], BF16, "xg%d" % u) for u in range(2)]
+        xi = [tile([P, JQ, PACK], BF16, "xi%d" % i) for i in range(4)]
         xq = tile([P, J], U32, "xq")
         xs = tile([P, J], U8, "xs")
-        for h in range(2):
-            cols = slice(h * JH, (h + 1) * JH)
-            nc.vector.quantize_mx(xq[:, cols].bitcast(FP8X4), xs[:, cols], xi[h][:].rearrange("p j t -> p (j t)"))
+
+        def weave(u, i, on_vector):
+            dst = xi[i][:, :, 2 * u : 2 * u + 2]
+            src = xg[u][:, :, pieces[i]].rearrange("p e j -> p j e")
+            if on_vector:
+                nc.vector.tensor_copy(dst, src)
+            else:
+                nc.scalar.copy(dst, src)
+
+        def quantize_x(i):
+            cols = pieces[i]
+            nc.vector.quantize_mx(xq[:, cols].bitcast(FP8X4), xs[:, cols], xi[i][:].rearrange("p j t -> p (j t)"))
+
+        for t in range(PACK):
+            nc.scalar.activation(xg[t // 2][:, t % 2, :], ta_sb[t][:].indirect(l1[:]), ACT.Copy, scale=ga_sb[:, t : t + 1])
+            if t == 1:
+                for i in range(4):
+                    weave(0, i, True)
+        for i in range(4):
+            weave(1, i, i < 2)
+        for i in range(4):
+            quantize_x(i)
 
         a_sb = [tile([P, J], F32, "a%d" % t, tag="a%d" % t) for t in range(PACK)]
 
-        def first_product(t, cols, bank):
-            acc = psum.tile([P, cols.stop - cols.start], F32, name="a_ps", tag="bank%d" % bank)
+        def first_product(acc, t, cols):
             nc.tensor.matmul_mx(
-                acc[:],
+                acc,
                 lhsT=wtw[:, 2 * P * t : 2 * P * (t + 1)].bitcast(FP4X4),
                 lhsT_scale=wts[:, P * t : P * (t + 1)],
                 rhs=xq[:, cols].bitcast(FP8X4),
@@ -143,29 +153,45 @@ def tile_picked_codes_store_one_weighedposting_outcomes_outmeet_kernel(
                 start=True,
                 stop=True,
             )
-            return acc
 
-        nc.scalar.copy(a_sb[0][:, 0:JH], first_product(0, slice(0, JH), 0)[:])
-        nc.vector.tensor_copy(a_sb[0][:, JH:J], first_product(0, slice(JH, J), 1)[:])
-        nc.vector.tensor_copy(a_sb[1][:], first_product(1, slice(0, J), 2)[:])
-        late = {t: first_product(t, slice(0, J), t + 1) for t in (2, 3)}
+        def bank(number, width):
+            return psum.tile([P, width], F32, name="acc", tag="bank%d" % number)
+
+        for i, cols in enumerate(pieces):
+            acc = bank(i, JQ)
+            first_product(acc[:], 0, cols)
+            if i == 3:
+                nc.vector.tensor_copy(a_sb[0][:, cols], acc[:])
+            else:
+                nc.scalar.copy(a_sb[0][:, cols], acc[:])
+        for h in range(2):
+            acc = bank(4 + h, JH)
+            for e in range(2):
+                first_product(acc[:, e * JQ : (e + 1) * JQ], 1, pieces[2 * h + e])
+            if h == 1:
+                nc.vector.tensor_copy(a_sb[1][:, JH:J], acc[:])
+            else:
+                nc.scalar.copy(a_sb[1][:, 0:JH], acc[:])
+        acc = bank(6, J)
+        first_product(acc[:], 2, slice(0, J))
+        nc.vector.tensor_copy(a_sb[2][:], acc[:])
+        acc_last = bank(7, J)
+        first_product(acc_last[:], 3, slice(0, J))
 
         h1 = [tile([P, S], F32, "h1_%d" % t, tag="h1_%d" % t) for t in range(PACK)]
         for t in range(PACK):
-            if t in late:
-                nc.scalar.copy(a_sb[t][:], late[t][:])
+            if t == PACK - 1:
+                nc.scalar.copy(a_sb[t][:], acc_last[:])
             nc.scalar.activation(h1[t][:], a_sb[t][:].indirect(l3[:]), ACT.Copy, scale=sa_sb[:, t : t + 1])
             src = h1[t]
-            if t in late:
+            if t > 0:
                 src = tile([P, S], F32, "kept%d" % t)
                 nc.scalar.activation(src[:], h1[t][:], ACT.Relu)
             nc.vector.tensor_copy(board[t][:].indirect(l4[:]), src[:])
-        g1 = []
-        for t, tag in ((0, "a3"), (1, "h1_3")):
-            g1.append(tile([P, C], F32, "g1_%d" % t, tag=tag))
-            nc.scalar.activation(g1[t][:], board[t][:], ACT.Relu)
-        g1.extend(board[2:])
-        hg_both = tile([P, 2, PACK, OH], BF16, "hg", tag="board1")
+        g1_first = tile([P, C], F32, "g1_first", tag="a3")
+        nc.scalar.activation(g1_first[:], board[0][:], ACT.Relu)
+        g1 = [g1_first] + board[1:]
+        hg_both = tile([P, 2, PACK, OH], BF16, "hg", tag="h1_3")
         hg = [hg_both[:, h] for h in range(2)]
         for t in range(PACK):
             for h in range(2):
@@ -175,16 +201,18 @@ def tile_picked_codes_store_one_weighedposting_outcomes_outmeet_kernel(
                     ACT.Copy,
                     scale=sb_sb[:, t : t + 1],
                 )
-
         hi_ = [tile([P, OH, PACK], BF16, "hi%d" % h) for h in range(2)]
         hq = tile([P, O], U32, "hq")
         hs = tile([P, O], U8, "hs")
         for h in range(2):
-            nc.vector.tensor_copy(hi_[h][:], hg[h].rearrange("p t o -> p o t"))
+            nc.vector.tensor_copy(
+                hi_[h][:].rearrange("p (c i) t -> p c t i", i=4), hg[h].rearrange("p t (c i) -> p c t i", i=4)
+            )
         for h in range(2):
             cols = slice(h * OH, (h + 1) * OH)
             nc.vector.quantize_mx(hq[:, cols].bitcast(FP8X4), hs[:, cols], hi_[h][:].rearrange("p o t -> p (o t)"))
 
+        halves = (slice(0, OH), slice(OH, O))
         for b in range(2):
             sides = (
                 (wbw[:, P * b : P * (b + 1)].bitcast(FP8X4), wbs, l6, so_sb),
@@ -192,10 +220,10 @@ def tile_picked_codes_store_one_weighedposting_outcomes_outmeet_kernel(
             )
             picked = []
             for m, (codes, plane, lst, weight) in enumerate(sides):
-                acc = psum.tile([P, O], F32, name="pq_ps", tag="bank%d" % ((5 + 2 * b + m) % 8))
-                for cols in (slice(0, OH), slice(OH, O)) if b == 0 else (slice(0, O),):
+
+                def second_product(acc, cols):
                     nc.tensor.matmul_mx(
-                        acc[:, cols],
+                        acc,
                         lhsT=codes,
                         lhsT_scale=plane[:, P * b : P * (b + 1)],
                         rhs=hq[:, cols].bitcast(FP8X4),
@@ -203,8 +231,21 @@ def tile_picked_codes_store_one_weighedposting_outcomes_outmeet_kernel(
                         start=True,
                         stop=True,
                     )
+
                 whole = tile([P, O], F32, "pq%d%d" % (b, m))
-                nc.vector.tensor_copy(whole[:], acc[:])
+                if b == 0 and m == 0:
+                    for h, cols in enumerate(halves):
+                        acc = bank(h, OH)
+                        second_product(acc[:], cols)
+                        if h == 0:
+                            nc.scalar.copy(whole[:, cols], acc[:])
+                        else:
+                            nc.vector.tensor_copy(whole[:, cols], acc[:])
+                else:
+                    acc = bank(1 + 2 * b + m, O)
+                    for cols in halves if b == 0 else (slice(0, O),):
+                        second_product(acc[:, cols], cols)
+                    nc.vector.tensor_copy(whole[:], acc[:])
                 part = tile([P, U], F32, "picked%d%d" % (b, m))
                 nc.scalar.activation(part[:], whole[:].indirect(lst[:]), ACT.Copy, scale=weight[:, b : b + 1])
                 picked.append(part)

@@ -56,7 +56,11 @@ def tile_picked_codes_store_one_weighedposting_outcomes_outmeet_kernel(
         ta_sb = [tile([P, T], F32, "ta%d" % t) for t in range(PACK)]
 
         wts_win = tile([P, F], U8, "wts_win")
-        nc.vector.memset(wts_win[:].bitcast(I32), 0)
+        nc.gpsimd.memset(wts_win[:].bitcast(I32), 0)
+        for q in range(4):
+            nc.gpsimd.dma_start(
+                wts_win[32 * q : 32 * q + 4, :].bitcast(I32), wt_scales[0, 4 * q : 4 * q + 4, :].bitcast(I32)
+            )
         wbs = tile([P, N], U8, "wbs")
         nc.vector.memset(wbs[:].bitcast(I32), 0)
         wos = tile([P, N], U8, "wos")
@@ -71,10 +75,6 @@ def tile_picked_codes_store_one_weighedposting_outcomes_outmeet_kernel(
         wtw_win = tile([P, F], U16, "wtw_win")
         nc.sync.dma_start(wtw_win[:].bitcast(I32), wt_words[0].bitcast(I32))
         l2 = load_list(offs2, "l2")
-        wts_stage = tile([P, 2, F // 4], I32, "wts_stage")
-        wts_src = wt_scales[0].bitcast(I32).rearrange("(g q r) c -> g r q c", g=2, q=2)
-        for g in range(2):
-            nc.sync.dma_start(wts_stage[64 * g : 64 * g + 4], wts_src[g])
         nc.sync.dma_start(ta_sb[1][:], ta_rows[1])
         nc.sync.dma_start(ta_sb[2][:], ta_rows[2])
         nc.sync.dma_start(ta_sb[3][:], ta_rows[3])
@@ -95,9 +95,6 @@ def tile_picked_codes_store_one_weighedposting_outcomes_outmeet_kernel(
         so_sb = load_blocks2(so, "so_sb")
         sp_sb = load_blocks2(sp, "sp_sb")
 
-        for q in range(4):
-            first = 64 * (q // 2)
-            nc.vector.tensor_copy(wts_win[32 * q : 32 * q + 4, :].bitcast(I32), wts_stage[first : first + 4, q % 2, :])
         wtw_g = tile([P, R], U16, "wtw_g")
         nc.vector.tensor_copy(wtw_g[:], wtw_win[:].indirect(l2[:]))
         wts_g = tile([P, R], U8, "wts_g")
@@ -119,9 +116,9 @@ def tile_picked_codes_store_one_weighedposting_outcomes_outmeet_kernel(
         xq = tile([P, J], U32, "xq")
         xs = tile([P, J], U8, "xs")
 
-        def weave(u, i, on_vector):
-            dst = xi[i][:, :, 2 * u : 2 * u + 2]
-            src = xg[u][:, :, pieces[i]].rearrange("p e j -> p j e")
+        def weave(u, i, lo, hi, on_vector):
+            dst = xi[i][:, lo:hi, 2 * u : 2 * u + 2]
+            src = xg[u][:, :, i * JQ + lo : i * JQ + hi].rearrange("p e j -> p j e")
             if on_vector:
                 nc.vector.tensor_copy(dst, src)
             else:
@@ -135,9 +132,12 @@ def tile_picked_codes_store_one_weighedposting_outcomes_outmeet_kernel(
             nc.scalar.activation(xg[t // 2][:, t % 2, :], ta_sb[t][:].indirect(l1[:]), ACT.Copy, scale=ga_sb[:, t : t + 1])
             if t == 1:
                 for i in range(4):
-                    weave(0, i, True)
-        for i in range(4):
-            weave(1, i, i < 2)
+                    weave(0, i, 0, JQ, True)
+        weave(1, 0, 0, JQ, True)
+        weave(1, 1, 0, JQ, True)
+        weave(1, 2, 0, JQ // 2, True)
+        weave(1, 2, JQ // 2, JQ, False)
+        weave(1, 3, 0, JQ, False)
         for i in range(4):
             quantize_x(i)
 
@@ -204,10 +204,11 @@ def tile_picked_codes_store_one_weighedposting_outcomes_outmeet_kernel(
         hi_ = [tile([P, OH, PACK], BF16, "hi%d" % h) for h in range(2)]
         hq = tile([P, O], U32, "hq")
         hs = tile([P, O], U8, "hs")
-        for h in range(2):
-            nc.vector.tensor_copy(
-                hi_[h][:].rearrange("p (c i) t -> p c t i", i=4), hg[h].rearrange("p t (c i) -> p c t i", i=4)
-            )
+        for u in range(2):
+            for h in range(2):
+                nc.vector.tensor_copy(
+                    hi_[h][:, :, 2 * u : 2 * u + 2], hg[h][:, 2 * u : 2 * u + 2, :].rearrange("p e o -> p o e")
+                )
         for h in range(2):
             cols = slice(h * OH, (h + 1) * OH)
             nc.vector.quantize_mx(hq[:, cols].bitcast(FP8X4), hs[:, cols], hi_[h][:].rearrange("p o t -> p (o t)"))

from contextlib import ExitStack

import concourse.mybir as mybir

K, J, R, T, F, O, C, S, N, U = 512, 512, 512, 2048, 1024, 256, 512, 256, 256, 128
FLOPS = 2 * K * R * J + 2 * 2 * R * N * O

F32 = mybir.dt.float32
BF16 = mybir.dt.bfloat16
I32 = mybir.dt.int32
U32 = mybir.dt.uint32
U16 = mybir.dt.uint16
U8 = mybir.dt.uint8
FP8X4 = mybir.dt.float8_e4m3fn_x4
FP4X4 = mybir.dt.float4_e2m1fn_x4
ACT = mybir.ActivationFunctionType
ALU = mybir.AluOpType

P = 128
PACK = 4
JH = J // 2
JQ = J // 4
SH = S // 2
OH = O // 2


def tile_picked_codes_store_one_weighedposting_outcomes_outmeet_kernel(
    tc, ta, ga, wt_words, wt_scales, sa, sb, wb_words, wb_scales, wo_words, wo_scales, so, sp,
    offs, offs2, offs3, offs4, offs5, offs6, offs7, out
):
    nc = tc.nc
    with ExitStack() as ctx:
        sb_pool = ctx.enter_context(tc.tile_pool(name="keep", bufs=1))
        psum = ctx.enter_context(tc.psum_pool(name="psum", bufs=1))

        def tile(shape, dtype, name, tag=""):
            return sb_pool.tile(shape, dtype, name=name, tag=tag, align_bytes=64)

        def load_list(src, name):
            lst = tile(list(src.shape), U16, name)
            nc.sync.dma_start(lst[:], src)
            return lst

        def load_rows4(src, name):
            col = tile([P, PACK], F32, name)
            nc.sync.dma_start(col[:], src.rearrange("(p t) o -> p (t o)", t=PACK))
            return col

        def load_blocks2(src, name):
            col = tile([P, 2], F32, name)
            with nc.allow_non_contiguous_dma(reason="one value a partition and block"):
                nc.sync.dma_start(col[:], src.rearrange("(b p) o -> p (b o)", b=2))
            return col

        ta_rows = ta.rearrange("(p t) c -> t p c", t=PACK)
        ta_sb = [tile([P, T], F32, "ta%d" % t) for t in range(PACK)]

        wts_win = tile([P, F], U8, "wts_win")
        nc.gpsimd.memset(wts_win[:].bitcast(I32), 0)
        for q in range(4):
            nc.gpsimd.dma_start(
                wts_win[32 * q : 32 * q + 4, :].bitcast(I32), wt_scales[0, 4 * q : 4 * q + 4, :].bitcast(I32)
            )
        wbs = tile([P, N], U8, "wbs")
        nc.vector.memset(wbs[:].bitcast(I32), 0)
        wos = tile([P, N], U8, "wos")
        nc.vector.memset(wos[:].bitcast(I32), 0)
        board = [tile([P, C], F32, "board%d" % t, tag="board%d" % t) for t in range(PACK)]
        for t in range(PACK):
            nc.vector.memset(board[t][:], 0.0)

        nc.sync.dma_start(ta_sb[0][:], ta_rows[0])
        l1 = load_list(offs, "l1")
        ga_sb = load_rows4(ga, "ga_sb")
        wtw_win = tile([P, F], U16, "wtw_win")
        nc.sync.dma_start(wtw_win[:].bitcast(I32), wt_words[0].bitcast(I32))
        l2 = load_list(offs2, "l2")
        nc.sync.dma_start(ta_sb[1][:], ta_rows[1])
        nc.sync.dma_start(ta_sb[2][:], ta_rows[2])
        nc.sync.dma_start(ta_sb[3][:], ta_rows[3])
        l3 = load_list(offs3, "l3")
        sa_sb = load_rows4(sa, "sa_sb")
        l4 = load_list(offs4, "l4")
        l5 = load_list(offs5, "l5")
        sb_sb = load_rows4(sb, "sb_sb")
        wbw = tile([P, N], U32, "wbw")
        nc.sync.dma_start(wbw[:].bitcast(I32), wb_words[0].rearrange("p n t -> p (n t)").bitcast(I32))
        wow = tile([P, 2 * N], U8, "wow")
        nc.sync.dma_start(wow[:].bitcast(I32), wo_words[0].bitcast(I32))
        for plane, src in ((wbs, wb_scales), (wos, wo_scales)):
            for q in range(4):
                nc.sync.dma_start(plane[32 * q : 32 * q + 4, :].bitcast(I32), src[0, 4 * q : 4 * q + 4, :].bitcast(I32))
        l6 = load_list(offs6, "l6")
        l7 = load_list(offs7, "l7")
        so_sb = load_blocks2(so, "so_sb")
        sp_sb = load_blocks2(sp, "sp_sb")

        wtw_g = tile([P, R], U16, "wtw_g")
        nc.vector.tensor_copy(wtw_g[:], wtw_win[:].indirect(l2[:]))
        wts_g = tile([P, R], U8, "wts_g")
        nc.vector.tensor_copy(wts_g[:], wts_win[:].indirect(l2[:]))
        wtw = tile([P, 2 * R], U8, "wtw")
        nc.vector.tensor_copy(
            wtw[:].rearrange("p (t m b) -> p t m b", t=PACK, b=2),
            wtw_g[:].bitcast(U8).rearrange("p (m t b) -> p t m b", t=PACK, b=2),
        )
        wts = tile([P, R], U8, "wts")
        nc.vector.tensor_copy(
            wts[:].rearrange("p (t m) -> p t m", t=PACK),
            wts_g[:].rearrange("p (m t) -> p t m", t=PACK),
        )

        pieces = [slice(i * JQ, (i + 1) * JQ) for i in range(4)]
        xg = [tile([P, 2, J], BF16, "xg%d" % u) for u in range(2)]
        xi = [tile([P, JQ, PACK], BF16, "xi%d" % i) for i in range(4)]
        xq = tile([P, J], U32, "xq")
        xs = tile([P, J], U8, "xs")

        def weave(u, i, lo, hi, on_vector):
            dst = xi[i][:, lo:hi, 2 * u : 2 * u + 2]
            src = xg[u][:, :, i * JQ + lo : i * JQ + hi].rearrange("p e j -> p j e")
            if on_vector:
                nc.vector.tensor_copy(dst, src)
            else:
                nc.scalar.copy(dst, src)

        def quantize_x(i):
            cols = pieces[i]
            nc.vector.quantize_mx(xq[:, cols].bitcast(FP8X4), xs[:, cols], xi[i][:].rearrange("p j t -> p (j t)"))

        for t in range(PACK):
            nc.scalar.activation(xg[t // 2][:, t % 2, :], ta_sb[t][:].indirect(l1[:]), ACT.Copy, scale=ga_sb[:, t : t + 1])
            if t == 1:
                for i in range(4):
                    weave(0, i, 0, JQ, True)
        weave(1, 0, 0, JQ, True)
        weave(1, 1, 0, JQ, True)
        weave(1, 2, 0, JQ // 2, True)
        weave(1, 2, JQ // 2, JQ, False)
        weave(1, 3, 0, JQ, False)
        for i in range(4):
            quantize_x(i)

        a_sb = [tile([P, J], F32, "a%d" % t, tag="a%d" % t) for t in range(PACK)]

        def first_product(acc, t, cols):
            nc.tensor.matmul_mx(
                acc,
                lhsT=wtw[:, 2 * P * t : 2 * P * (t + 1)].bitcast(FP4X4),
                lhsT_scale=wts[:, P * t : P * (t + 1)],
                rhs=xq[:, cols].bitcast(FP8X4),
                rhs_scale=xs[:, cols],
                start=True,
                stop=True,
            )

        def bank(number, width):
            return psum.tile([P, width], F32, name="acc", tag="bank%d" % number)

        for i, cols in enumerate(pieces):
            acc = bank(i, JQ)
            first_product(acc[:], 0, cols)
            if i == 3:
                nc.vector.tensor_copy(a_sb[0][:, cols], acc[:])
            else:
                nc.scalar.copy(a_sb[0][:, cols], acc[:])
        for h in range(2):
            acc = bank(4 + h, JH)
            for e in range(2):
                first_product(acc[:, e * JQ : (e + 1) * JQ], 1, pieces[2 * h + e])
            if h == 1:
                nc.vector.tensor_copy(a_sb[1][:, JH:J], acc[:])
            else:
                nc.scalar.copy(a_sb[1][:, 0:JH], acc[:])
        acc = bank(6, J)
        first_product(acc[:], 2, slice(0, J))
        nc.vector.tensor_copy(a_sb[2][:], acc[:])
        acc_last = bank(7, J)
        first_product(acc_last[:], 3, slice(0, J))

        h1 = [tile([P, S], F32, "h1_%d" % t, tag="h1_%d" % t) for t in range(PACK)]
        for t in range(PACK):
            if t == PACK - 1:
                nc.scalar.copy(a_sb[t][:], acc_last[:])
            nc.scalar.activation(h1[t][:], a_sb[t][:].indirect(l3[:]), ACT.Copy, scale=sa_sb[:, t : t + 1])
            src = h1[t]
            if t > 0:
                src = tile([P, S], F32, "kept%d" % t)
                nc.scalar.activation(src[:], h1[t][:], ACT.Relu)
            nc.vector.tensor_copy(board[t][:].indirect(l4[:]), src[:])
        g1_first = tile([P, C], F32, "g1_first", tag="a3")
        nc.scalar.activation(g1_first[:], board[0][:], ACT.Relu)
        g1 = [g1_first] + board[1:]
        hg_both = tile([P, 2, PACK, OH], BF16, "hg", tag="h1_3")
        hg = [hg_both[:, h] for h in range(2)]
        for t in range(PACK):
            for h in range(2):
                nc.scalar.activation(
                    hg[h][:, t, :],
                    g1[t][:].indirect(l5[:, h * OH // 16 : (h + 1) * OH // 16]),
                    ACT.Copy,
                    scale=sb_sb[:, t : t + 1],
                )
        hi_ = [tile([P, OH, PACK], BF16, "hi%d" % h) for h in range(2)]
        hq = tile([P, O], U32, "hq")
        hs = tile([P, O], U8, "hs")
        for u in range(2):
            for h in range(2):
                nc.vector.tensor_copy(
                    hi_[h][:, :, 2 * u : 2 * u + 2], hg[h][:, 2 * u : 2 * u + 2, :].rearrange("p e o -> p o e")
                )
        for h in range(2):
            cols = slice(h * OH, (h + 1) * OH)
            nc.vector.quantize_mx(hq[:, cols].bitcast(FP8X4), hs[:, cols], hi_[h][:].rearrange("p o t -> p (o t)"))

        halves = (slice(0, OH), slice(OH, O))
        for b in range(2):
            sides = (
                (wbw[:, P * b : P * (b + 1)].bitcast(FP8X4), wbs, l6, so_sb),
                (wow[:, 2 * P * b : 2 * P * (b + 1)].bitcast(FP4X4), wos, l7, sp_sb),
            )
            picked = []
            for m, (codes, plane, lst, weight) in enumerate(sides):

                def second_product(acc, cols):
                    nc.tensor.matmul_mx(
                        acc,
                        lhsT=codes,
                        lhsT_scale=plane[:, P * b : P * (b + 1)],
                        rhs=hq[:, cols].bitcast(FP8X4),
                        rhs_scale=hs[:, cols],
                        start=True,
                        stop=True,
                    )

                whole = tile([P, O], F32, "pq%d%d" % (b, m))
                if b == 0 and m == 0:
                    for h, cols in enumerate(halves):
                        acc = bank(h, OH)
                        second_product(acc[:], cols)
                        if h == 0:
                            nc.scalar.copy(whole[:, cols], acc[:])
                        else:
                            nc.vector.tensor_copy(whole[:, cols], acc[:])
                else:
                    acc = bank(1 + 2 * b + m, O)
                    for cols in halves if b == 0 else (slice(0, O),):
                        second_product(acc[:, cols], cols)
                    nc.vector.tensor_copy(whole[:], acc[:])
                part = tile([P, U], F32, "picked%d%d" % (b, m))
                nc.scalar.activation(part[:], whole[:].indirect(lst[:]), ACT.Copy, scale=weight[:, b : b + 1])
                picked.append(part)
            y = tile([P, U], F32, "y%d" % b)
            nc.vector.tensor_tensor(y[:], picked[0][:], picked[1][:], ALU.subtract)
            nc.sync.dma_start(out[P * b : P * (b + 1), :], y[:])
